import numpy as np
import ml_dtypes


def mxq(x, axis, fmt="e4m3"):
    dtype, down = {"e4m3": (ml_dtypes.float8_e4m3fn, 7), "e5m2": (ml_dtypes.float8_e5m2, 14)}[fmt]
    v = np.moveaxis(np.asarray(x, np.float32).astype(ml_dtypes.bfloat16).astype(np.float64), axis, -1)
    blocks = v.reshape(v.shape[:-1] + (-1, 32))
    amax = np.abs(blocks).max(-1, keepdims=True)
    byte = np.maximum(np.where(amax > 0, np.frexp(amax)[1] - 1 + 127, 0) - down, 1)
    scale = np.exp2(byte - 127.0)
    codes = (blocks / scale).astype(np.float32).astype(dtype).astype(np.float64)
    return np.moveaxis((codes * scale).reshape(v.shape), -1, axis)


WIDE = False


def mx_kscale(k):
    if not WIDE:
        return np.ones(k)
    levels = np.array([30, -30])
    if k % 512:
        return np.exp2(np.random.permutation(np.resize(levels, k // 32))).repeat(32)
    a = np.empty((k // 512, 16))
    for p in range(k // 512):
        a[p, :8] = np.random.permutation(np.resize(levels, 8))
        for g in range(8):
            far = levels[np.abs(levels - a[p, g]) >= 10]
            a[p, g + 8] = far[np.random.randint(len(far))]
    return np.exp2(a.ravel()).repeat(32)


BF16 = ml_dtypes.bfloat16


def bf(x):
    return np.asarray(x, np.float32).astype(BF16)


def f64(x):
    return np.asarray(x).astype(np.float64)


M, B, S, Q, P = 512, 4, 512, 1024, 512


def setup_inputs():
    s = mx_kscale(B * S).reshape(B, S)
    t = mx_kscale(B * Q)
    t_dealt = t.reshape(Q, B).T[:, None, :]
    t_plain = t.reshape(B, Q)[:, :, None]
    return {"dy": bf(np.random.standard_normal((M, S * B)) * s.T.reshape(-1)),
            "w2": bf(np.random.standard_normal((B, S, Q)) / np.sqrt(S) / s[:, :, None] * t_dealt),
            "z": bf(np.random.standard_normal((M, B * Q))),
            "v": bf(np.random.standard_normal((M, B * Q))),
            "wa": bf(np.random.standard_normal((B, Q, P)) / np.sqrt(Q) / t_plain),
            "wb": bf(np.random.standard_normal((B, Q, P)) / np.sqrt(Q) / t_plain)}


def reference(dy, w2, z, v, wa, wb):
    g = f64(dy).reshape(M, S, B).transpose(2, 0, 1)
    e = mxq(g, 2, "e4m3") @ mxq(f64(w2), 1, "e4m3")
    dh = e.transpose(1, 2, 0).reshape(M, Q * B)
    zz = f64(z)
    sg = 1.0 / (1.0 + np.exp(-zz))
    dz = dh * f64(v) * (sg * (1.0 + zz * (1.0 - sg)))
    dv = dh * (zz * sg)
    dzb = dz.reshape(M, B, Q).transpose(1, 0, 2)
    dvb = dv.reshape(M, B, Q).transpose(1, 0, 2)
    da = mxq(dzb, 2, "e5m2") @ mxq(f64(wa), 1, "e4m3")
    db = mxq(dvb, 2, "e5m2") @ mxq(f64(wb), 1, "e4m3")
    return (da + db).transpose(1, 0, 2).reshape(M, B * P)

@@ -1,0 +1,354 @@
+from contextlib import ExitStack
+
+import concourse.mybir as mybir
+from concourse.masks import make_identity
+
+M, B, S, Q, C = 512, 4, 512, 1024, 512
+
+F32 = mybir.dt.float32
+BF16 = mybir.dt.bfloat16
+U32 = mybir.dt.uint32
+U8 = mybir.dt.uint8
+E4M3 = mybir.dt.float8_e4m3fn_x4
+E5M2 = mybir.dt.float8_e5m2_x4
+ADD = mybir.AluOpType.add
+SUB = mybir.AluOpType.subtract
+MULT = mybir.AluOpType.mult
+ACT = mybir.ActivationFunctionType
+
+FLOPS = 2 * M * B * S * Q + 2 * 2 * M * B * Q * C
+
+P = 128
+PACK = 4
+TOK = 256
+UNITS = [(k, mp, h) for k in range(B) for mp in range(2) for h in range(2)]
+LAG = 2
+
+
+def tile_monarch_glu_input_gradient_f3_kernel(tc, dy, w2, z, v, wa, wb, out):
+    nc = tc.nc
+    with ExitStack() as ctx:
+        const = ctx.enter_context(tc.tile_pool(name="const", bufs=1))
+        raw = ctx.enter_context(tc.tile_pool(name="raw", bufs=2))
+        inter = ctx.enter_context(tc.tile_pool(name="inter", bufs=3))
+        quant = ctx.enter_context(tc.tile_pool(name="quant", bufs=2))
+        mid = ctx.enter_context(tc.tile_pool(name="mid", bufs=2))
+        psum = ctx.enter_context(tc.psum_pool(name="psum", bufs=2))
+        ctx.enter_context(tc.manual_schedule())
+
+        dy_raw, w2_raw, big_raw, zv_raw = {}, {}, {}, {}
+
+        def load_dy(mp):
+            t = raw.tile([P, 2, B * S], BF16, name="dyraw", bufs=2)
+            for a in range(2):
+                r0 = TOK * mp + P * a
+                nc.sync.dma_start(out=t[:, a, :], in_=dy[r0 : r0 + P, :])
+            dy_raw[mp] = t
+
+        def load_zv(g):
+            k, mp = divmod(g, 2)
+            pair = []
+            for nm, src in (("zraw", z), ("vraw", v)):
+                t = raw.tile([P, 2, Q], BF16, name=nm, bufs=3)
+                nc.sync.dma_start(
+                    out=t[:],
+                    in_=src[TOK * mp : TOK * (mp + 1), Q * k : Q * (k + 1)].rearrange("(a p) n -> p a n", p=P),
+                )
+                pair.append(t)
+            zv_raw[g] = pair
+
+        def load_w2(k, l):
+            t = raw.tile([P, PACK, TOK], BF16, name="w2raw", bufs=6)
+            nc.sync.dma_start(out=t[:], in_=w2[l, :, TOK * k : TOK * (k + 1)].rearrange("(p t) r -> p t r", t=PACK))
+            w2_raw[k, l] = t
+
+        def load_big(k, u):
+            h, ab = divmod(u, 2)
+            t = raw.tile([P, PACK, C], BF16, name="bigraw", bufs=5)
+            src = (wa, wb)[ab]
+            nc.sync.dma_start(out=t[:], in_=src[k, 512 * h : 512 * (h + 1), :].rearrange("(p t) c -> p t c", t=PACK))
+            big_raw[k, u] = t
+
+        def interleave(engine, dst, src):
+            d = dst.rearrange("p (c i) t -> p c t i", i=4)
+            s = src.rearrange("p t (c i) -> p c t i", i=4)
+            if engine == "act":
+                nc.scalar.copy(out=d, in_=s)
+            elif engine == "vec":
+                nc.vector.tensor_copy(out=d, in_=s)
+            else:
+                nc.gpsimd.tensor_scalar(d, s, 1.0, 0.0, MULT, ADD)
+
+        w2_int, big_int, dy_int = {}, {}, {}
+        w2_codes, w2_scales, big_q = {}, {}, {}
+        dy_codes = const.tile([P, B, M], U32, align_bytes=64, name="dycodes")
+        dy_scales = const.tile([P, B, M], U8, align_bytes=64, name="dyscales")
+
+        def copy_w2(k, l, engine):
+            t = inter.tile([P, TOK, PACK], BF16, align_bytes=64, name="w2int", bufs=5)
+            interleave(engine, t[:], w2_raw[k, l][:])
+            w2_int[k, l] = t
+
+        def quant_w2(k, l):
+            if l == 0:
+                w2_codes[k] = quant.tile([P, B, TOK], U32, align_bytes=64, name="w2codes", bufs=2)
+                w2_scales[k] = quant.tile([P, B, TOK], U8, align_bytes=64, name="w2scales", bufs=2)
+            nc.vector.quantize_mx(
+                out=w2_codes[k][:, l, :].bitcast(E4M3),
+                scales=w2_scales[k][:, l, :],
+                in_=w2_int[k, l][:].rearrange("p r t -> p (r t)"),
+            )
+
+        def copy_big(k, u, shares):
+            t = inter.tile([P, C, PACK], BF16, align_bytes=64, name="bigint", bufs=4)
+            c0 = 0
+            for engine, width in shares:
+                interleave(engine, t[:, c0 : c0 + width, :], big_raw[k, u][:, :, c0 : c0 + width])
+                c0 += width
+            big_int[k, u] = t
+
+        def quant_big(k, u):
+            codes = quant.tile([P, C], U32, align_bytes=64, name="bigcodes", bufs=8)
+            scales = quant.tile([P, C], U8, align_bytes=64, name="bigscales", bufs=8)
+            nc.vector.quantize_mx(
+                out=codes[:].bitcast(E4M3), scales=scales[:], in_=big_int[k, u][:].rearrange("p c t -> p (c t)")
+            )
+            big_q[k, u] = (codes, scales)
+
+        def transpose_dy(mp, l, tag):
+            t = psum.tile([P, PACK, TOK], BF16, name=tag, bufs=2)
+            for a in range(2):
+                for j in range(PACK):
+                    nc.tensor.transpose(
+                        t[:, j, P * a : P * (a + 1)],
+                        dy_raw[mp][:, a, PACK * j + l : B * S : PACK * B],
+                        ident[:],
+                    )
+            return t
+
+        def copy_dy(mp, l, bank, engine):
+            t = inter.tile([P, TOK, PACK], BF16, align_bytes=64, name="dyint", bufs=4)
+            interleave(engine, t[:], bank[:])
+            dy_int[mp, l] = t
+
+        def quant_dy(mp, l):
+            cols = slice(TOK * mp, TOK * (mp + 1))
+            nc.vector.quantize_mx(
+                out=dy_codes[:, l, cols].bitcast(E4M3),
+                scales=dy_scales[:, l, cols],
+                in_=dy_int[mp, l][:].rearrange("p m t -> p (m t)"),
+            )
+
+        zT, vT, th, sp, hh, ee, dh = {}, {}, {}, {}, {}, {}, {}
+        dzb, dvb, dzq, dvq, acc = {}, {}, {}, {}, {}
+
+        def transpose_zv(i):
+            k, mp, h = UNITS[i]
+            pair = zv_raw[2 * k + mp]
+            for src, tag, keep in ((pair[0], "zT", zT), (pair[1], "vT", vT)):
+                t = psum.tile([P, PACK, TOK], BF16, name=tag, bufs=2)
+                for a in range(2):
+                    for l in range(PACK):
+                        nc.tensor.transpose(
+                            t[:, l, P * a : P * (a + 1)],
+                            src[:, a, 512 * h + l : 512 * (h + 1) : PACK],
+                            ident[:],
+                        )
+                keep[i] = t
+
+        def act_sp(i):
+            t = mid.tile([P, TOK, PACK], F32, name="sp", bufs=3)
+            nc.scalar.activation(out=t[:], in_=zT[i][:].rearrange("p l m -> p m l"), func=ACT.Silu, scale=-1.0)
+            sp[i] = t
+
+        def act_th(i):
+            t = mid.tile([P, TOK, PACK], F32, name="th", bufs=3)
+            nc.scalar.activation(out=t[:], in_=zT[i][:].rearrange("p l m -> p m l"), func=ACT.Tanh, scale=0.5)
+            th[i] = t
+
+        def vec_h(i):
+            t = mid.tile([P, TOK, PACK], F32, name="hh", bufs=2)
+            nc.vector.scalar_tensor_tensor(
+                out=t[:], in0=sp[i][:], scalar=1.0, in1=vT[i][:].rearrange("p l m -> p m l"), op0=SUB, op1=MULT
+            )
+            hh[i] = t
+
+        def stage1(i):
+            k, mp, h = UNITS[i]
+            for a in range(2):
+                t = psum.tile([P, PACK, P], F32, name="dh", bufs=2)
+                m0 = TOK * mp + P * a
+                for l in range(PACK):
+                    nc.tensor.matmul_mx(
+                        out=t[:, l, :],
+                        lhsT=w2_codes[k][:, l, P * h : P * (h + 1)].bitcast(E4M3),
+                        lhsT_scale=w2_scales[k][:, l, P * h : P * (h + 1)],
+                        rhs=dy_codes[:, l, m0 : m0 + P].bitcast(E4M3),
+                        rhs_scale=dy_scales[:, l, m0 : m0 + P],
+                        start=True,
+                        stop=True,
+                    )
+                dh[i, a] = t
+
+        def vec_e(i):
+            t = mid.tile([P, TOK, PACK], F32, name="ee", bufs=2)
+            for a in range(2):
+                rows = slice(P * a, P * (a + 1))
+                nc.vector.scalar_tensor_tensor(
+                    out=t[:, rows, :], in0=th[i][:, rows, :], scalar=1.0,
+                    in1=dh[i, a][:].rearrange("p l m -> p m l"), op0=ADD, op1=MULT,
+                )
+            ee[i] = t
+
+        def gp_dz(i):
+            t = mid.tile([P, TOK, PACK], BF16, align_bytes=64, name="dzb", bufs=2)
+            nc.gpsimd.tensor_tensor(out=t[:], in0=ee[i][:], in1=hh[i][:], op=MULT)
+            dzb[i] = t
+
+        def vec_dv(i):
+            t = mid.tile([P, TOK, PACK], BF16, align_bytes=64, name="dvb", bufs=2)
+            nc.vector.scalar_tensor_tensor(
+                out=t[:], in0=ee[i][:], scalar=-1.0, in1=zT[i][:].rearrange("p l m -> p m l"), op0=MULT, op1=MULT
+            )
+            dvb[i] = t
+
+        def quant_mid(i, src, keep, nm):
+            codes = quant.tile([P, TOK], U32, align_bytes=64, name=nm + "codes", bufs=4)
+            scales = quant.tile([P, TOK], U8, align_bytes=64, name=nm + "scales", bufs=4)
+            nc.vector.quantize_mx(
+                out=codes[:].bitcast(E5M2), scales=scales[:], in_=src[i][:].rearrange("p m l -> p (m l)")
+            )
+            keep[i] = (codes, scales)
+
+        def stage2(i):
+            k, mp, h = UNITS[i]
+            if h == 0:
+                acc[k, mp] = [psum.tile([P, C], F32, name="dx", bufs=2) for a in range(2)]
+            for ab, keep in ((1, dvq), (0, dzq)):
+                for a in range(2):
+                    codes, scales = keep[i]
+                    w_codes, w_scales = big_q[k, 2 * h + ab]
+                    cols = slice(P * a, P * (a + 1))
+                    nc.tensor.matmul_mx(
+                        out=acc[k, mp][a][:],
+                        lhsT=codes[:, cols].bitcast(E5M2),
+                        lhsT_scale=scales[:, cols],
+                        rhs=w_codes[:].bitcast(E4M3),
+                        rhs_scale=w_scales[:],
+                        start=(h == 0 and ab == 1),
+                        stop=(h == 1 and ab == 0),
+                    )
+
+        def finish(i, engines=("act", "act")):
+            k, mp, h = UNITS[i]
+            if h == 0:
+                return
+            for a in range(2):
+                t = mid.tile([P, C], F32, name="dxo", bufs=4)
+                if engines[a] == "act":
+                    nc.scalar.activation(out=t[:], in_=acc[k, mp][a][:], func=ACT.Copy, scale=-0.5)
+                else:
+                    nc.vector.tensor_scalar(t[:], acc[k, mp][a][:], -0.5, None, MULT)
+                r0 = TOK * mp + P * a
+                nc.sync.dma_start(out=out[r0 : r0 + P, C * k : C * (k + 1)], in_=t[:])
+
+        big_at = {(0, 0): 0, (0, 1): 0, (0, 2): 1, (0, 3): 1}
+        w2_at = {(1, 0): 0, (1, 1): 0, (1, 2): 1, (1, 3): 2}
+        for k in range(1, B):
+            for u in range(4):
+                big_at[k, u] = 4 * k - 2 + u
+                if k > 1:
+                    w2_at[k, u] = 4 * k - 5 + u
+        needs = []
+        for g in range(2, 2 * B):
+            needs.append((2 * g - 2, 0, load_zv, (g,)))
+        for key, j in big_at.items():
+            needs.append((j, 1, load_big, key))
+        for key, j in w2_at.items():
+            needs.append((j, 2, load_w2, key))
+        needs.sort(key=lambda n: (n[0], n[1], n[3]))
+
+        def emit_loads(upto):
+            while needs and needs[0][0] <= upto:
+                n = needs[0]
+                needs.remove(n)
+                n[2](*n[3])
+
+        load_dy(0)
+        for l in range(B):
+            load_w2(0, l)
+        load_zv(0)
+        load_dy(1)
+        load_zv(1)
+        emit_loads(2)
+
+        ident = const.tile([P, P], BF16, name="ident")
+        make_identity(nc, ident[:])
+        warm = const.tile([P, 1], F32, name="warm")
+        nc.vector.memset(warm[:], 0.0)
+        warm2 = const.tile([P, 1], F32, name="warm2")
+        nc.scalar.activation(out=warm2[:], in_=warm[:], func=ACT.Silu)
+
+        banks = [transpose_dy(0, l, ("zT", "vT")[l % 2]) for l in range(B)]
+        for l in range(B):
+            copy_dy(0, l, banks[l], ("act", "vec")[l % 2])
+        for l in range(B):
+            copy_w2(0, l, ("act", "vec", "gp", "vec")[l])
+        for l in range(B):
+            quant_dy(0, l)
+        for l in range(B):
+            quant_w2(0, l)
+        for i in range(2):
+            transpose_zv(i)
+            act_sp(i)
+            act_th(i)
+        stage1(0)
+        vec_h(0)
+
+        n_units = len(UNITS)
+        w2_todo, big_todo = [], []
+        for j in range(n_units):
+            for key in w2_todo:
+                quant_w2(*key)
+            w2_todo = [key for key, it in w2_at.items() if it == j]
+            big_now = [key for key, it in big_at.items() if it == j]
+            if j >= LAG:
+                stage2(j - LAG)
+            vec_e(j)
+            gp_dz(j)
+            if j == 0:
+                banks = [transpose_dy(1, l, "dx") for l in range(2)]
+                copy_dy(1, 0, banks[0], "act")
+                copy_dy(1, 1, banks[1], "vec")
+                banks = [transpose_dy(1, l, "dx") for l in range(2, 4)]
+                copy_dy(1, 2, banks[0], "act")
+                copy_dy(1, 3, banks[1], "vec")
+                for l in range(B):
+                    quant_dy(1, l)
+            if j + 1 < n_units:
+                stage1(j + 1)
+            if big_now:
+                copy_big(*big_now[0], [("act", C)])
+            if j + 1 < n_units:
+                vec_h(j + 1)
+            vec_dv(j)
+            if j >= LAG:
+                finish(j - LAG)
+            if j + 2 < n_units:
+                transpose_zv(j + 2)
+            for key in big_todo:
+                quant_big(*key)
+            for key in w2_todo:
+                copy_w2(*key, "vec")
+            quant_mid(j, dvb, dvq, "dv")
+            quant_mid(j, dzb, dzq, "dz")
+            if j + 2 < n_units:
+                act_sp(j + 2)
+                act_th(j + 2)
+            for key in big_now[1:]:
+                copy_big(*key, [("gp", C)])
+            big_todo = big_now
+            emit_loads(j + 3)
+        for i in range(n_units - LAG, n_units):
+            stage2(i)
+            finish(i, ("act", "vec"))

@@ -21,8 +21,11 @@ FLOPS = 2 * M * B * S * Q + 2 * 2 * M * B * Q * C
 P = 128
 PACK = 4
 TOK = 256
+BUFS = {"zT": 3, "vT": 2, "dh": 2, "dx": 1}
 UNITS = [(k, mp, h) for k in range(B) for mp in range(2) for h in range(2)]
-LAG = 2
+LAG = 4
+W2_SPLIT = (("gp", 128), ("vec", 128))
+BIG_SPLIT = (("act", 512),)
 
 
 def tile_monarch_glu_input_gradient_f3_kernel(tc, dy, w2, z, v, wa, wb, out):
@@ -84,10 +87,15 @@ def tile_monarch_glu_input_gradient_f3_kernel(tc, dy, w2, z, v, wa, wb, out):
         dy_codes = const.tile([P, B, M], U32, align_bytes=64, name="dycodes")
         dy_scales = const.tile([P, B, M], U8, align_bytes=64, name="dyscales")
 
-        def copy_w2(k, l, engine):
-            t = inter.tile([P, TOK, PACK], BF16, align_bytes=64, name="w2int", bufs=5)
-            interleave(engine, t[:], w2_raw[k, l][:])
-            w2_int[k, l] = t
+        def copy_w2(k, l, shares, c0=0):
+            if c0 == 0:
+                w2_int[k, l] = inter.tile(
+                    [P, TOK, PACK], BF16, align_bytes=64, name="w2int" if 4 * k + l > 4 else "w2int0", bufs=1 if 4 * k + l > 4 else 4
+                )
+            for engine, width in shares:
+                cols = slice(c0, c0 + width)
+                interleave(engine, w2_int[k, l][:, cols, :], w2_raw[k, l][:, :, cols])
+                c0 += width
 
         def quant_w2(k, l):
             if l == 0:
@@ -116,7 +124,7 @@ def tile_monarch_glu_input_gradient_f3_kernel(tc, dy, w2, z, v, wa, wb, out):
             big_q[k, u] = (codes, scales)
 
         def transpose_dy(mp, l, tag):
-            t = psum.tile([P, PACK, TOK], BF16, name=tag, bufs=2)
+            t = psum.tile([P, PACK, TOK], BF16, name=tag, bufs=BUFS[tag])
             for a in range(2):
                 for j in range(PACK):
                     nc.tensor.transpose(
@@ -146,7 +154,7 @@ def tile_monarch_glu_input_gradient_f3_kernel(tc, dy, w2, z, v, wa, wb, out):
             k, mp, h = UNITS[i]
             pair = zv_raw[2 * k + mp]
             for src, tag, keep in ((pair[0], "zT", zT), (pair[1], "vT", vT)):
-                t = psum.tile([P, PACK, TOK], BF16, name=tag, bufs=2)
+                t = psum.tile([P, PACK, TOK], BF16, name=tag, bufs=BUFS[tag])
                 for a in range(2):
                     for l in range(PACK):
                         nc.tensor.transpose(
@@ -200,9 +208,11 @@ def tile_monarch_glu_input_gradient_f3_kernel(tc, dy, w2, z, v, wa, wb, out):
                 )
             ee[i] = t
 
-        def gp_dz(i):
+        def make_dz(i, engines):
             t = mid.tile([P, TOK, PACK], BF16, align_bytes=64, name="dzb", bufs=2)
-            nc.gpsimd.tensor_tensor(out=t[:], in0=ee[i][:], in1=hh[i][:], op=MULT)
+            for a in range(2):
+                rows = slice(P * a, P * (a + 1))
+                engines[a].tensor_tensor(out=t[:, rows, :], in0=ee[i][:, rows, :], in1=hh[i][:, rows, :], op=MULT)
             dzb[i] = t
 
         def vec_dv(i):
@@ -213,24 +223,24 @@ def tile_monarch_glu_input_gradient_f3_kernel(tc, dy, w2, z, v, wa, wb, out):
             dvb[i] = t
 
         def quant_mid(i, src, keep, nm):
-            codes = quant.tile([P, TOK], U32, align_bytes=64, name=nm + "codes", bufs=4)
-            scales = quant.tile([P, TOK], U8, align_bytes=64, name=nm + "scales", bufs=4)
+            codes = quant.tile([P, TOK], U32, align_bytes=64, name=nm + "codes", bufs=6)
+            scales = quant.tile([P, TOK], U8, align_bytes=64, name=nm + "scales", bufs=6)
             nc.vector.quantize_mx(
                 out=codes[:].bitcast(E5M2), scales=scales[:], in_=src[i][:].rearrange("p m l -> p (m l)")
             )
             keep[i] = (codes, scales)
 
-        def stage2(i):
-            k, mp, h = UNITS[i]
-            if h == 0:
-                acc[k, mp] = [psum.tile([P, C], F32, name="dx", bufs=2) for a in range(2)]
-            for ab, keep in ((1, dvq), (0, dzq)):
-                for a in range(2):
-                    codes, scales = keep[i]
+        def stage2(g, a, hs, tag="dx"):
+            k = g // 2
+            if hs[0] == 0:
+                acc[g, a] = psum.tile([P, C], F32, name=tag, bufs=BUFS[tag])
+            cols = slice(P * a, P * (a + 1))
+            for h in hs:
+                for ab, keep in ((1, dvq), (0, dzq)):
+                    codes, scales = keep[2 * g + h]
                     w_codes, w_scales = big_q[k, 2 * h + ab]
-                    cols = slice(P * a, P * (a + 1))
                     nc.tensor.matmul_mx(
-                        out=acc[k, mp][a][:],
+                        out=acc[g, a][:],
                         lhsT=codes[:, cols].bitcast(E5M2),
                         lhsT_scale=scales[:, cols],
                         rhs=w_codes[:].bitcast(E4M3),
@@ -239,26 +249,22 @@ def tile_monarch_glu_input_gradient_f3_kernel(tc, dy, w2, z, v, wa, wb, out):
                         stop=(h == 1 and ab == 0),
                     )
 
-        def finish(i, engines=("act", "act")):
-            k, mp, h = UNITS[i]
-            if h == 0:
-                return
-            for a in range(2):
-                t = mid.tile([P, C], F32, name="dxo", bufs=4)
-                if engines[a] == "act":
-                    nc.scalar.activation(out=t[:], in_=acc[k, mp][a][:], func=ACT.Copy, scale=-0.5)
-                else:
-                    nc.vector.tensor_scalar(t[:], acc[k, mp][a][:], -0.5, None, MULT)
-                r0 = TOK * mp + P * a
-                nc.sync.dma_start(out=out[r0 : r0 + P, C * k : C * (k + 1)], in_=t[:])
+        def finish(g, a, engine="act"):
+            k, mp = divmod(g, 2)
+            t = mid.tile([P, C], F32, name="dxo", bufs=4)
+            if engine == "act":
+                nc.scalar.activation(out=t[:], in_=acc[g, a][:], func=ACT.Copy, scale=-0.5)
+            else:
+                nc.vector.tensor_scalar(t[:], acc[g, a][:], -0.5, None, MULT)
+            r0 = TOK * mp + P * a
+            nc.sync.dma_start(out=out[r0 : r0 + P, C * k : C * (k + 1)], in_=t[:])
 
-        big_at = {(0, 0): 0, (0, 1): 0, (0, 2): 1, (0, 3): 1}
-        w2_at = {(1, 0): 0, (1, 1): 0, (1, 2): 1, (1, 3): 2}
-        for k in range(1, B):
+        big_at, w2_at = {}, {}
+        for k in range(B):
             for u in range(4):
-                big_at[k, u] = 4 * k - 2 + u
-                if k > 1:
-                    w2_at[k, u] = 4 * k - 5 + u
+                big_at[k, u] = max(0, 4 * k - 1 + u)
+                if k > 0:
+                    w2_at[k, u] = max(0, 4 * k - 5 + u)
         needs = []
         for g in range(2, 2 * B):
             needs.append((2 * g - 2, 0, load_zv, (g,)))
@@ -293,7 +299,7 @@ def tile_monarch_glu_input_gradient_f3_kernel(tc, dy, w2, z, v, wa, wb, out):
         for l in range(B):
             copy_dy(0, l, banks[l], ("act", "vec")[l % 2])
         for l in range(B):
-            copy_w2(0, l, ("act", "vec", "gp", "vec")[l])
+            copy_w2(0, l, ((("act", "vec", "gp", "vec")[l], TOK),))
         for l in range(B):
             quant_dy(0, l)
         for l in range(B):
@@ -304,51 +310,73 @@ def tile_monarch_glu_input_gradient_f3_kernel(tc, dy, w2, z, v, wa, wb, out):
             act_th(i)
         stage1(0)
         vec_h(0)
+        for l in (0, 1):
+            copy_dy(1, l, transpose_dy(1, l, ("dx", "zT")[l]), "act")
 
         n_units = len(UNITS)
         w2_todo, big_todo = [], []
         for j in range(n_units):
+            last = j == n_units - 1
             for key in w2_todo:
                 quant_w2(*key)
             w2_todo = [key for key, it in w2_at.items() if it == j]
             big_now = [key for key, it in big_at.items() if it == j]
+            if last:
+                for key in big_todo:
+                    quant_big(*key)
+                big_todo = []
+            if 0 < j < n_units - 2:
+                transpose_zv(j + 2)
+            g, a = divmod(j - LAG, 2)
             if j >= LAG:
-                stage2(j - LAG)
+                stage2(g, a, (0, 1))
             vec_e(j)
-            gp_dz(j)
-            if j == 0:
-                banks = [transpose_dy(1, l, "dx") for l in range(2)]
-                copy_dy(1, 0, banks[0], "act")
-                copy_dy(1, 1, banks[1], "vec")
-                banks = [transpose_dy(1, l, "dx") for l in range(2, 4)]
-                copy_dy(1, 2, banks[0], "act")
-                copy_dy(1, 3, banks[1], "vec")
-                for l in range(B):
-                    quant_dy(1, l)
-            if j + 1 < n_units:
+            if j > 0:
+                for key in w2_todo:
+                    copy_w2(*key, W2_SPLIT[:1])
+            if not last:
+                make_dz(j, (nc.gpsimd, nc.gpsimd))
                 stage1(j + 1)
-            if big_now:
-                copy_big(*big_now[0], [("act", C)])
-            if j + 1 < n_units:
+            if j == 0:
+                for key in w2_todo:
+                    copy_w2(*key, W2_SPLIT[:1])
+            if j == 0:
+                for l in (2, 3):
+                    copy_dy(1, l, transpose_dy(1, l, "dx"), "act")
+            if not last:
                 vec_h(j + 1)
             vec_dv(j)
+            if last:
+                make_dz(j, (nc.gpsimd, nc.vector))
+            if j == 0:
+                transpose_zv(2)
+                act_sp(2)
+                act_th(2)
+            for key in big_now:
+                copy_big(*key, BIG_SPLIT)
+            if 0 < j < n_units - 2:
+                act_sp(j + 2)
+                act_th(j + 2)
             if j >= LAG:
-                finish(j - LAG)
-            if j + 2 < n_units:
-                transpose_zv(j + 2)
+                finish(g, a)
             for key in big_todo:
                 quant_big(*key)
             for key in w2_todo:
-                copy_w2(*key, "vec")
+                copy_w2(*key, W2_SPLIT[1:], W2_SPLIT[0][1])
             quant_mid(j, dvb, dvq, "dv")
             quant_mid(j, dzb, dzq, "dz")
-            if j + 2 < n_units:
-                act_sp(j + 2)
-                act_th(j + 2)
-            for key in big_now[1:]:
-                copy_big(*key, [("gp", C)])
+            if j == 0:
+                for l in range(B):
+                    quant_dy(1, l)
             big_todo = big_now
             emit_loads(j + 3)
-        for i in range(n_units - LAG, n_units):
-            stage2(i)
-            finish(i, ("act", "vec"))
+        stage2(6, 0, (0, 1))
+        stage2(6, 1, (0, 1), "vT")
+        stage2(7, 0, (0,), "zT")
+        stage2(7, 1, (0,), "zT")
+        finish(6, 0)
+        finish(6, 1)
+        stage2(7, 0, (1,))
+        stage2(7, 1, (1,))
+        finish(7, 0, "act")
+        finish(7, 1, "vec")

@@ -24,8 +24,8 @@ TOK = 256
 BUFS = {"zT": 3, "vT": 2, "dh": 2, "dx": 1}
 UNITS = [(k, mp, h) for k in range(B) for mp in range(2) for h in range(2)]
 LAG = 4
-W2_SPLIT = (("gp", 128), ("vec", 128))
-BIG_SPLIT = (("act", 512),)
+W2_GP = 128
+BIG_ACT = 480
 
 
 def tile_monarch_glu_input_gradient_f3_kernel(tc, dy, w2, z, v, wa, wb, out):
@@ -72,20 +72,25 @@ def tile_monarch_glu_input_gradient_f3_kernel(tc, dy, w2, z, v, wa, wb, out):
             nc.sync.dma_start(out=t[:], in_=src[k, 512 * h : 512 * (h + 1), :].rearrange("(p t) c -> p t c", t=PACK))
             big_raw[k, u] = t
 
-        def interleave(engine, dst, src):
+        def interleave(engine, dst, src, sign):
+            if engine == "gp":
+                nc.gpsimd.tensor_scalar(dst, src.rearrange("p t c -> p c t"), sign, 0.0, MULT, ADD)
+                return
             d = dst.rearrange("p (c i) t -> p c t i", i=4)
             s = src.rearrange("p t (c i) -> p c t i", i=4)
-            if engine == "act":
+            if engine == "act" and sign > 0:
                 nc.scalar.copy(out=d, in_=s)
-            elif engine == "vec":
+            elif engine == "act":
+                nc.scalar.mul(out=d, in_=s, mul=sign)
+            elif sign > 0:
                 nc.vector.tensor_copy(out=d, in_=s)
             else:
-                nc.gpsimd.tensor_scalar(d, s, 1.0, 0.0, MULT, ADD)
+                nc.vector.tensor_scalar(d, s, sign, None, MULT)
 
         w2_int, big_int, dy_int = {}, {}, {}
         w2_codes, w2_scales, big_q = {}, {}, {}
-        dy_codes = const.tile([P, B, M], U32, align_bytes=64, name="dycodes")
-        dy_scales = const.tile([P, B, M], U8, align_bytes=64, name="dyscales")
+        dy_codes = const.tile([P, 2, B, TOK], U32, align_bytes=64, name="dycodes")
+        dy_scales = const.tile([P, 2, B, TOK], U8, align_bytes=64, name="dyscales")
 
         def copy_w2(k, l, shares, c0=0):
             if c0 == 0:
@@ -94,7 +99,7 @@ def tile_monarch_glu_input_gradient_f3_kernel(tc, dy, w2, z, v, wa, wb, out):
                 )
             for engine, width in shares:
                 cols = slice(c0, c0 + width)
-                interleave(engine, w2_int[k, l][:, cols, :], w2_raw[k, l][:, :, cols])
+                interleave(engine, w2_int[k, l][:, cols, :], w2_raw[k, l][:, :, cols], 1.0)
                 c0 += width
 
         def quant_w2(k, l):
@@ -107,13 +112,12 @@ def tile_monarch_glu_input_gradient_f3_kernel(tc, dy, w2, z, v, wa, wb, out):
                 in_=w2_int[k, l][:].rearrange("p r t -> p (r t)"),
             )
 
-        def copy_big(k, u, shares):
-            t = inter.tile([P, C, PACK], BF16, align_bytes=64, name="bigint", bufs=4)
-            c0 = 0
-            for engine, width in shares:
-                interleave(engine, t[:, c0 : c0 + width, :], big_raw[k, u][:, :, c0 : c0 + width])
-                c0 += width
-            big_int[k, u] = t
+        def copy_big(k, u, engine, c0, c1):
+            if c0 == 0:
+                big_int[k, u] = inter.tile([P, C, PACK], BF16, align_bytes=64, name="bigint", bufs=4)
+            if c1 > c0:
+                sign = 1.0 if u % 2 else -1.0
+                interleave(engine, big_int[k, u][:, c0:c1, :], big_raw[k, u][:, :, c0:c1], sign)
 
         def quant_big(k, u):
             codes = quant.tile([P, C], U32, align_bytes=64, name="bigcodes", bufs=8)
@@ -123,28 +127,29 @@ def tile_monarch_glu_input_gradient_f3_kernel(tc, dy, w2, z, v, wa, wb, out):
             )
             big_q[k, u] = (codes, scales)
 
-        def transpose_dy(mp, l, tag):
-            t = psum.tile([P, PACK, TOK], BF16, name=tag, bufs=BUFS[tag])
-            for a in range(2):
-                for j in range(PACK):
-                    nc.tensor.transpose(
-                        t[:, j, P * a : P * (a + 1)],
-                        dy_raw[mp][:, a, PACK * j + l : B * S : PACK * B],
-                        ident[:],
-                    )
+        def transpose_dy(mp, a, lh, tag):
+            t = psum.tile([P, PACK, P], F32, name=tag, bufs=BUFS[tag])
+            words = dy_raw[mp][:].bitcast(F32)
+            for j in range(PACK):
+                nc.tensor.transpose(t[:, j, :], words[:, a, 2 * j + lh : B * S // 2 : 8], ident[:])
             return t
 
-        def copy_dy(mp, l, bank, engine):
-            t = inter.tile([P, TOK, PACK], BF16, align_bytes=64, name="dyint", bufs=4)
-            interleave(engine, t[:], bank[:])
-            dy_int[mp, l] = t
+        def copy_dy(mp, a, lh, bank, engine):
+            if a == 0:
+                dy_int[mp, lh] = inter.tile([P, 2, TOK, PACK], BF16, align_bytes=64, name="dyint", bufs=4)
+            d = dy_int[mp, lh][:, :, P * a : P * (a + 1), :]
+            s = bank[:].bitcast(BF16).rearrange("p t (m e) -> p e m t", e=2)
+            if engine == "act":
+                nc.scalar.copy(out=d, in_=s)
+            else:
+                nc.vector.tensor_copy(out=d, in_=s)
 
-        def quant_dy(mp, l):
-            cols = slice(TOK * mp, TOK * (mp + 1))
+        def quant_dy(mp, lh):
+            ls = slice(2 * lh, 2 * lh + 2)
             nc.vector.quantize_mx(
-                out=dy_codes[:, l, cols].bitcast(E4M3),
-                scales=dy_scales[:, l, cols],
-                in_=dy_int[mp, l][:].rearrange("p m t -> p (m t)"),
+                out=dy_codes[:, mp, ls, :].rearrange("p l m -> p (l m)").bitcast(E4M3),
+                scales=dy_scales[:, mp, ls, :].rearrange("p l m -> p (l m)"),
+                in_=dy_int[mp, lh][:].rearrange("p e m t -> p (e m t)"),
             )
 
         zT, vT, th, sp, hh, ee, dh = {}, {}, {}, {}, {}, {}, {}
@@ -154,30 +159,33 @@ def tile_monarch_glu_input_gradient_f3_kernel(tc, dy, w2, z, v, wa, wb, out):
             k, mp, h = UNITS[i]
             pair = zv_raw[2 * k + mp]
             for src, tag, keep in ((pair[0], "zT", zT), (pair[1], "vT", vT)):
-                t = psum.tile([P, PACK, TOK], BF16, name=tag, bufs=BUFS[tag])
+                t = psum.tile([P, 2, TOK], F32, name=tag, bufs=BUFS[tag])
+                words = src[:].bitcast(F32)
                 for a in range(2):
-                    for l in range(PACK):
+                    for u in range(2):
                         nc.tensor.transpose(
-                            t[:, l, P * a : P * (a + 1)],
-                            src[:, a, 512 * h + l : 512 * (h + 1) : PACK],
+                            t[:, u, P * a : P * (a + 1)],
+                            words[:, a, 256 * h + u : 256 * (h + 1) : 2],
                             ident[:],
                         )
                 keep[i] = t
 
         def act_sp(i):
-            t = mid.tile([P, TOK, PACK], F32, name="sp", bufs=3)
-            nc.scalar.activation(out=t[:], in_=zT[i][:].rearrange("p l m -> p m l"), func=ACT.Silu, scale=-1.0)
+            t = mid.tile([P, 2, 2 * TOK], F32, name="sp", bufs=3)
+            nc.scalar.activation(out=t[:], in_=zT[i][:].bitcast(BF16), func=ACT.Silu, scale=-1.0)
             sp[i] = t
 
         def act_th(i):
-            t = mid.tile([P, TOK, PACK], F32, name="th", bufs=3)
-            nc.scalar.activation(out=t[:], in_=zT[i][:].rearrange("p l m -> p m l"), func=ACT.Tanh, scale=0.5)
+            t = mid.tile([P, TOK, 2, 2], F32, name="th", bufs=3)
+            nc.scalar.activation(
+                out=t[:], in_=zT[i][:].bitcast(BF16).rearrange("p u (m e) -> p m u e", e=2), func=ACT.Tanh, scale=0.5
+            )
             th[i] = t
 
         def vec_h(i):
-            t = mid.tile([P, TOK, PACK], F32, name="hh", bufs=2)
+            t = mid.tile([P, 2, 2 * TOK], F32, name="hh", bufs=2)
             nc.vector.scalar_tensor_tensor(
-                out=t[:], in0=sp[i][:], scalar=1.0, in1=vT[i][:].rearrange("p l m -> p m l"), op0=SUB, op1=MULT
+                out=t[:], in0=sp[i][:], scalar=1.0, in1=vT[i][:].bitcast(BF16), op0=SUB, op1=MULT
             )
             hh[i] = t
 
@@ -185,40 +193,49 @@ def tile_monarch_glu_input_gradient_f3_kernel(tc, dy, w2, z, v, wa, wb, out):
             k, mp, h = UNITS[i]
             for a in range(2):
                 t = psum.tile([P, PACK, P], F32, name="dh", bufs=2)
-                m0 = TOK * mp + P * a
+                cols = slice(P * a, P * (a + 1))
                 for l in range(PACK):
                     nc.tensor.matmul_mx(
                         out=t[:, l, :],
                         lhsT=w2_codes[k][:, l, P * h : P * (h + 1)].bitcast(E4M3),
                         lhsT_scale=w2_scales[k][:, l, P * h : P * (h + 1)],
-                        rhs=dy_codes[:, l, m0 : m0 + P].bitcast(E4M3),
-                        rhs_scale=dy_scales[:, l, m0 : m0 + P],
+                        rhs=dy_codes[:, mp, l, cols].bitcast(E4M3),
+                        rhs_scale=dy_scales[:, mp, l, cols],
                         start=True,
                         stop=True,
                     )
                 dh[i, a] = t
 
         def vec_e(i):
-            t = mid.tile([P, TOK, PACK], F32, name="ee", bufs=2)
+            t = mid.tile([P, TOK, 2, 2], F32, name="ee", bufs=2)
             for a in range(2):
                 rows = slice(P * a, P * (a + 1))
                 nc.vector.scalar_tensor_tensor(
-                    out=t[:, rows, :], in0=th[i][:, rows, :], scalar=1.0,
-                    in1=dh[i, a][:].rearrange("p l m -> p m l"), op0=ADD, op1=MULT,
+                    out=t[:, rows].rearrange("p m u e -> p m (u e)"),
+                    in0=th[i][:, rows].rearrange("p m u e -> p m (u e)"),
+                    scalar=1.0,
+                    in1=dh[i, a][:].rearrange("p l m -> p m l"),
+                    op0=ADD,
+                    op1=MULT,
                 )
             ee[i] = t
 
         def make_dz(i, engines):
-            t = mid.tile([P, TOK, PACK], BF16, align_bytes=64, name="dzb", bufs=2)
+            t = mid.tile([P, TOK, 2, 2], BF16, align_bytes=64, name="dzb", bufs=2)
             for a in range(2):
                 rows = slice(P * a, P * (a + 1))
-                engines[a].tensor_tensor(out=t[:, rows, :], in0=ee[i][:, rows, :], in1=hh[i][:, rows, :], op=MULT)
+                engines[a].tensor_tensor(
+                    out=t[:, rows],
+                    in0=ee[i][:, rows],
+                    in1=hh[i][:, :, 2 * P * a : 2 * P * (a + 1)].rearrange("p u (m e) -> p m u e", e=2),
+                    op=MULT,
+                )
             dzb[i] = t
 
         def vec_dv(i):
-            t = mid.tile([P, TOK, PACK], BF16, align_bytes=64, name="dvb", bufs=2)
-            nc.vector.scalar_tensor_tensor(
-                out=t[:], in0=ee[i][:], scalar=-1.0, in1=zT[i][:].rearrange("p l m -> p m l"), op0=MULT, op1=MULT
+            t = mid.tile([P, TOK, 2, 2], BF16, align_bytes=64, name="dvb", bufs=2)
+            nc.vector.tensor_tensor(
+                out=t[:], in0=ee[i][:], in1=zT[i][:].bitcast(BF16).rearrange("p u (m e) -> p m u e", e=2), op=MULT
             )
             dvb[i] = t
 
@@ -226,7 +243,7 @@ def tile_monarch_glu_input_gradient_f3_kernel(tc, dy, w2, z, v, wa, wb, out):
             codes = quant.tile([P, TOK], U32, align_bytes=64, name=nm + "codes", bufs=6)
             scales = quant.tile([P, TOK], U8, align_bytes=64, name=nm + "scales", bufs=6)
             nc.vector.quantize_mx(
-                out=codes[:].bitcast(E5M2), scales=scales[:], in_=src[i][:].rearrange("p m l -> p (m l)")
+                out=codes[:].bitcast(E5M2), scales=scales[:], in_=src[i][:].rearrange("p m u e -> p (m u e)")
             )
             keep[i] = (codes, scales)
 
@@ -253,9 +270,9 @@ def tile_monarch_glu_input_gradient_f3_kernel(tc, dy, w2, z, v, wa, wb, out):
             k, mp = divmod(g, 2)
             t = mid.tile([P, C], F32, name="dxo", bufs=4)
             if engine == "act":
-                nc.scalar.activation(out=t[:], in_=acc[g, a][:], func=ACT.Copy, scale=-0.5)
+                nc.scalar.activation(out=t[:], in_=acc[g, a][:], func=ACT.Copy, scale=0.5)
             else:
-                nc.vector.tensor_scalar(t[:], acc[g, a][:], -0.5, None, MULT)
+                nc.vector.tensor_scalar(t[:], acc[g, a][:], 0.5, None, MULT)
             r0 = TOK * mp + P * a
             nc.sync.dma_start(out=out[r0 : r0 + P, C * k : C * (k + 1)], in_=t[:])
 
@@ -288,20 +305,20 @@ def tile_monarch_glu_input_gradient_f3_kernel(tc, dy, w2, z, v, wa, wb, out):
         load_zv(1)
         emit_loads(2)
 
-        ident = const.tile([P, P], BF16, name="ident")
+        ident = const.tile([P, P], F32, name="ident")
         make_identity(nc, ident[:])
         warm = const.tile([P, 1], F32, name="warm")
         nc.vector.memset(warm[:], 0.0)
         warm2 = const.tile([P, 1], F32, name="warm2")
         nc.scalar.activation(out=warm2[:], in_=warm[:], func=ACT.Silu)
 
-        banks = [transpose_dy(0, l, ("zT", "vT")[l % 2]) for l in range(B)]
-        for l in range(B):
-            copy_dy(0, l, banks[l], ("act", "vec")[l % 2])
+        pieces = [(a, lh) for a in range(2) for lh in range(2)]
+        for a, lh in pieces:
+            copy_dy(0, a, lh, transpose_dy(0, a, lh, ("zT", "vT")[lh]), ("vec", "act")[lh])
         for l in range(B):
             copy_w2(0, l, ((("act", "vec", "gp", "vec")[l], TOK),))
-        for l in range(B):
-            quant_dy(0, l)
+        for lh in range(2):
+            quant_dy(0, lh)
         for l in range(B):
             quant_w2(0, l)
         for i in range(2):
@@ -310,8 +327,8 @@ def tile_monarch_glu_input_gradient_f3_kernel(tc, dy, w2, z, v, wa, wb, out):
             act_th(i)
         stage1(0)
         vec_h(0)
-        for l in (0, 1):
-            copy_dy(1, l, transpose_dy(1, l, ("dx", "zT")[l]), "act")
+        for a, lh in pieces[:2]:
+            copy_dy(1, a, lh, transpose_dy(1, a, lh, ("dx", "zT")[lh]), "act")
 
         n_units = len(UNITS)
         w2_todo, big_todo = [], []
@@ -333,16 +350,16 @@ def tile_monarch_glu_input_gradient_f3_kernel(tc, dy, w2, z, v, wa, wb, out):
             vec_e(j)
             if j > 0:
                 for key in w2_todo:
-                    copy_w2(*key, W2_SPLIT[:1])
+                    copy_w2(*key, (("gp", W2_GP),))
             if not last:
                 make_dz(j, (nc.gpsimd, nc.gpsimd))
                 stage1(j + 1)
             if j == 0:
                 for key in w2_todo:
-                    copy_w2(*key, W2_SPLIT[:1])
+                    copy_w2(*key, (("gp", W2_GP),))
             if j == 0:
-                for l in (2, 3):
-                    copy_dy(1, l, transpose_dy(1, l, "dx"), "act")
+                for a, lh in pieces[2:]:
+                    copy_dy(1, a, lh, transpose_dy(1, a, lh, "dx"), "act")
             if not last:
                 vec_h(j + 1)
             vec_dv(j)
@@ -353,21 +370,23 @@ def tile_monarch_glu_input_gradient_f3_kernel(tc, dy, w2, z, v, wa, wb, out):
                 act_sp(2)
                 act_th(2)
             for key in big_now:
-                copy_big(*key, BIG_SPLIT)
+                copy_big(*key, "act", 0, BIG_ACT)
             if 0 < j < n_units - 2:
                 act_sp(j + 2)
                 act_th(j + 2)
             if j >= LAG:
                 finish(g, a)
-            for key in big_todo:
-                quant_big(*key)
+            for key in big_now:
+                copy_big(*key, "vec", BIG_ACT, C)
             for key in w2_todo:
-                copy_w2(*key, W2_SPLIT[1:], W2_SPLIT[0][1])
+                copy_w2(*key, (("vec", TOK - W2_GP),), W2_GP)
             quant_mid(j, dvb, dvq, "dv")
             quant_mid(j, dzb, dzq, "dz")
+            for key in big_todo:
+                quant_big(*key)
             if j == 0:
-                for l in range(B):
-                    quant_dy(1, l)
+                for lh in range(2):
+                    quant_dy(1, lh)
             big_todo = big_now
             emit_loads(j + 3)
         stage2(6, 0, (0, 1))

@@ -24,8 +24,8 @@ TOK = 256
 BUFS = {"zT": 3, "vT": 2, "dh": 2, "dx": 1}
 UNITS = [(k, mp, h) for k in range(B) for mp in range(2) for h in range(2)]
 LAG = 4
-W2_GP = 128
-BIG_ACT = 480
+W2_GP = 64
+BIG_ACT = 496
 
 
 def tile_monarch_glu_input_gradient_f3_kernel(tc, dy, w2, z, v, wa, wb, out):
@@ -183,7 +183,7 @@ def tile_monarch_glu_input_gradient_f3_kernel(tc, dy, w2, z, v, wa, wb, out):
             th[i] = t
 
         def vec_h(i):
-            t = mid.tile([P, 2, 2 * TOK], F32, name="hh", bufs=2)
+            t = mid.tile([P, 2, 2 * TOK], F32, name="hh", bufs=3)
             nc.vector.scalar_tensor_tensor(
                 out=t[:], in0=sp[i][:], scalar=1.0, in1=vT[i][:].bitcast(BF16), op0=SUB, op1=MULT
             )
@@ -221,13 +221,14 @@ def tile_monarch_glu_input_gradient_f3_kernel(tc, dy, w2, z, v, wa, wb, out):
             ee[i] = t
 
         def make_dz(i, engines):
-            t = mid.tile([P, TOK, 2, 2], BF16, align_bytes=64, name="dzb", bufs=2)
-            for a in range(2):
-                rows = slice(P * a, P * (a + 1))
-                engines[a].tensor_tensor(
+            t = mid.tile([P, TOK, 2, 2], BF16, align_bytes=64, name="dzb", bufs=1)
+            step = P if len(engines) == 2 else TOK
+            for a, engine in enumerate(engines):
+                rows = slice(step * a, step * (a + 1))
+                engine.tensor_tensor(
                     out=t[:, rows],
                     in0=ee[i][:, rows],
-                    in1=hh[i][:, :, 2 * P * a : 2 * P * (a + 1)].rearrange("p u (m e) -> p m u e", e=2),
+                    in1=hh[i][:, :, 2 * step * a : 2 * step * (a + 1)].rearrange("p u (m e) -> p m u e", e=2),
                     op=MULT,
                 )
             dzb[i] = t
@@ -239,22 +240,26 @@ def tile_monarch_glu_input_gradient_f3_kernel(tc, dy, w2, z, v, wa, wb, out):
             )
             dvb[i] = t
 
-        def quant_mid(i, src, keep, nm):
+        def quant_mid(i, src, keep, nm, pieces=1):
             codes = quant.tile([P, TOK], U32, align_bytes=64, name=nm + "codes", bufs=6)
             scales = quant.tile([P, TOK], U8, align_bytes=64, name=nm + "scales", bufs=6)
-            nc.vector.quantize_mx(
-                out=codes[:].bitcast(E5M2), scales=scales[:], in_=src[i][:].rearrange("p m u e -> p (m u e)")
-            )
+            step = TOK // pieces
+            for c in range(0, TOK, step):
+                nc.vector.quantize_mx(
+                    out=codes[:, c : c + step].bitcast(E5M2),
+                    scales=scales[:, c : c + step],
+                    in_=src[i][:, c : c + step].rearrange("p m u e -> p (m u e)"),
+                )
             keep[i] = (codes, scales)
 
-        def stage2(g, a, hs, tag="dx"):
+        def stage2(g, a, hs, tag="dx", parts=(1, 0)):
             k = g // 2
-            if hs[0] == 0:
+            if hs[0] == 0 and parts[0] == 1:
                 acc[g, a] = psum.tile([P, C], F32, name=tag, bufs=BUFS[tag])
             cols = slice(P * a, P * (a + 1))
             for h in hs:
-                for ab, keep in ((1, dvq), (0, dzq)):
-                    codes, scales = keep[2 * g + h]
+                for ab in parts:
+                    codes, scales = (dzq, dvq)[ab][2 * g + h]
                     w_codes, w_scales = big_q[k, 2 * h + ab]
                     nc.tensor.matmul_mx(
                         out=acc[g, a][:],
@@ -279,16 +284,16 @@ def tile_monarch_glu_input_gradient_f3_kernel(tc, dy, w2, z, v, wa, wb, out):
         big_at, w2_at = {}, {}
         for k in range(B):
             for u in range(4):
-                big_at[k, u] = max(0, 4 * k - 1 + u)
+                big_at[k, u] = 4 * k - 1 + u if k > 0 else min(u, 2)
                 if k > 0:
                     w2_at[k, u] = max(0, 4 * k - 5 + u)
         needs = []
         for g in range(2, 2 * B):
             needs.append((2 * g - 2, 0, load_zv, (g,)))
         for key, j in big_at.items():
-            needs.append((j, 1, load_big, key))
+            needs.append((j, 2, load_big, key))
         for key, j in w2_at.items():
-            needs.append((j, 2, load_w2, key))
+            needs.append((j, 1, load_w2, key))
         needs.sort(key=lambda n: (n[0], n[1], n[3]))
 
         def emit_loads(upto):
@@ -315,11 +320,14 @@ def tile_monarch_glu_input_gradient_f3_kernel(tc, dy, w2, z, v, wa, wb, out):
         pieces = [(a, lh) for a in range(2) for lh in range(2)]
         for a, lh in pieces:
             copy_dy(0, a, lh, transpose_dy(0, a, lh, ("zT", "vT")[lh]), ("vec", "act")[lh])
-        for l in range(B):
-            copy_w2(0, l, ((("act", "vec", "gp", "vec")[l], TOK),))
+            if lh == 1:
+                copy_w2(0, a, ((("vec", "gp")[a], TOK),))
+        copy_w2(0, 2, (("act", TOK),))
+        quant_w2(0, 0)
+        copy_w2(0, 3, (("vec", TOK),))
         for lh in range(2):
             quant_dy(0, lh)
-        for l in range(B):
+        for l in range(1, B):
             quant_w2(0, l)
         for i in range(2):
             transpose_zv(i)
@@ -331,12 +339,10 @@ def tile_monarch_glu_input_gradient_f3_kernel(tc, dy, w2, z, v, wa, wb, out):
             copy_dy(1, a, lh, transpose_dy(1, a, lh, ("dx", "zT")[lh]), "act")
 
         n_units = len(UNITS)
-        w2_todo, big_todo = [], []
+        big_todo = []
         for j in range(n_units):
             last = j == n_units - 1
-            for key in w2_todo:
-                quant_w2(*key)
-            w2_todo = [key for key, it in w2_at.items() if it == j]
+            w2_now = [key for key, it in w2_at.items() if it == j]
             big_now = [key for key, it in big_at.items() if it == j]
             if last:
                 for key in big_todo:
@@ -349,22 +355,17 @@ def tile_monarch_glu_input_gradient_f3_kernel(tc, dy, w2, z, v, wa, wb, out):
                 stage2(g, a, (0, 1))
             vec_e(j)
             if j > 0:
-                for key in w2_todo:
+                make_dz(j - 1, (nc.gpsimd,))
+                for key in w2_now:
                     copy_w2(*key, (("gp", W2_GP),))
             if not last:
-                make_dz(j, (nc.gpsimd, nc.gpsimd))
                 stage1(j + 1)
             if j == 0:
-                for key in w2_todo:
-                    copy_w2(*key, (("gp", W2_GP),))
-            if j == 0:
-                for a, lh in pieces[2:]:
-                    copy_dy(1, a, lh, transpose_dy(1, a, lh, "dx"), "act")
+                bank = transpose_dy(1, 1, 1, "vT")
+                copy_dy(1, 1, 0, transpose_dy(1, 1, 0, "dx"), "act")
             if not last:
                 vec_h(j + 1)
             vec_dv(j)
-            if last:
-                make_dz(j, (nc.gpsimd, nc.vector))
             if j == 0:
                 transpose_zv(2)
                 act_sp(2)
@@ -376,17 +377,26 @@ def tile_monarch_glu_input_gradient_f3_kernel(tc, dy, w2, z, v, wa, wb, out):
                 act_th(j + 2)
             if j >= LAG:
                 finish(g, a)
+            if j == 0:
+                copy_dy(1, 1, 1, bank, "vec")
+            for key in w2_now:
+                c0 = W2_GP if j > 0 else 0
+                copy_w2(*key, (("vec", TOK - c0),), c0)
             for key in big_now:
                 copy_big(*key, "vec", BIG_ACT, C)
-            for key in w2_todo:
-                copy_w2(*key, (("vec", TOK - W2_GP),), W2_GP)
             quant_mid(j, dvb, dvq, "dv")
-            quant_mid(j, dzb, dzq, "dz")
             for key in big_todo:
                 quant_big(*key)
+            for key in w2_now:
+                quant_w2(*key)
             if j == 0:
                 for lh in range(2):
-                    quant_dy(1, lh)
+                    quant_dy(1, 1 - lh)
+            if j > 0:
+                quant_mid(j - 1, dzb, dzq, "dz")
+            if last:
+                make_dz(j, (nc.vector,))
+                quant_mid(j, dzb, dzq, "dz", 2)
             big_todo = big_now
             emit_loads(j + 3)
         stage2(6, 0, (0, 1))
@@ -395,7 +405,8 @@ def tile_monarch_glu_input_gradient_f3_kernel(tc, dy, w2, z, v, wa, wb, out):
         stage2(7, 1, (0,), "zT")
         finish(6, 0)
         finish(6, 1)
-        stage2(7, 0, (1,))
-        stage2(7, 1, (1,))
+        for ab in (1, 0):
+            for a in range(2):
+                stage2(7, a, (1,), parts=(ab,))
         finish(7, 0, "act")
         finish(7, 1, "vec")

@@ -24,8 +24,10 @@ TOK = 256
 BUFS = {"zT": 3, "vT": 2, "dh": 2, "dx": 1}
 UNITS = [(k, mp, h) for k in range(B) for mp in range(2) for h in range(2)]
 LAG = 4
-W2_GP = 64
-BIG_ACT = 496
+PASSES = [(0, 1), (0, 0), (1, 1), (1, 0)]
+TAIL = 2
+W2_GP = 96
+BIG_ACT = 512
 
 
 def tile_monarch_glu_input_gradient_f3_kernel(tc, dy, w2, z, v, wa, wb, out):
@@ -220,18 +222,15 @@ def tile_monarch_glu_input_gradient_f3_kernel(tc, dy, w2, z, v, wa, wb, out):
                 )
             ee[i] = t
 
-        def make_dz(i, engines):
-            t = mid.tile([P, TOK, 2, 2], BF16, align_bytes=64, name="dzb", bufs=1)
-            step = P if len(engines) == 2 else TOK
-            for a, engine in enumerate(engines):
-                rows = slice(step * a, step * (a + 1))
-                engine.tensor_tensor(
-                    out=t[:, rows],
-                    in0=ee[i][:, rows],
-                    in1=hh[i][:, :, 2 * step * a : 2 * step * (a + 1)].rearrange("p u (m e) -> p m u e", e=2),
-                    op=MULT,
-                )
-            dzb[i] = t
+        def make_dz(i, name, engine, m0, m1):
+            if m0 == 0:
+                dzb[i] = mid.tile([P, TOK, 2, 2], BF16, align_bytes=64, name=name, bufs=1)
+            engine.tensor_tensor(
+                out=dzb[i][:, m0:m1],
+                in0=ee[i][:, m0:m1],
+                in1=hh[i][:, :, 2 * m0 : 2 * m1].rearrange("p u (m e) -> p m u e", e=2),
+                op=MULT,
+            )
 
         def vec_dv(i):
             t = mid.tile([P, TOK, 2, 2], BF16, align_bytes=64, name="dvb", bufs=2)
@@ -252,34 +251,36 @@ def tile_monarch_glu_input_gradient_f3_kernel(tc, dy, w2, z, v, wa, wb, out):
                 )
             keep[i] = (codes, scales)
 
-        def stage2(g, a, hs, tag="dx", parts=(1, 0)):
+        def stage2(g, a, passes, tag="dx"):
             k = g // 2
-            if hs[0] == 0 and parts[0] == 1:
+            if passes[0] == (0, 1):
                 acc[g, a] = psum.tile([P, C], F32, name=tag, bufs=BUFS[tag])
             cols = slice(P * a, P * (a + 1))
-            for h in hs:
-                for ab in parts:
-                    codes, scales = (dzq, dvq)[ab][2 * g + h]
-                    w_codes, w_scales = big_q[k, 2 * h + ab]
-                    nc.tensor.matmul_mx(
-                        out=acc[g, a][:],
-                        lhsT=codes[:, cols].bitcast(E5M2),
-                        lhsT_scale=scales[:, cols],
-                        rhs=w_codes[:].bitcast(E4M3),
-                        rhs_scale=w_scales[:],
-                        start=(h == 0 and ab == 1),
-                        stop=(h == 1 and ab == 0),
-                    )
+            for h, ab in passes:
+                codes, scales = (dzq, dvq)[ab][2 * g + h]
+                w_codes, w_scales = big_q[k, 2 * h + ab]
+                nc.tensor.matmul_mx(
+                    out=acc[g, a][:],
+                    lhsT=codes[:, cols].bitcast(E5M2),
+                    lhsT_scale=scales[:, cols],
+                    rhs=w_codes[:].bitcast(E4M3),
+                    rhs_scale=w_scales[:],
+                    start=((h, ab) == (0, 1)),
+                    stop=((h, ab) == (1, 0)),
+                )
 
-        def finish(g, a, engine="act"):
+        def finish(g, a, engine="act", pieces=1):
             k, mp = divmod(g, 2)
             t = mid.tile([P, C], F32, name="dxo", bufs=4)
-            if engine == "act":
-                nc.scalar.activation(out=t[:], in_=acc[g, a][:], func=ACT.Copy, scale=0.5)
-            else:
-                nc.vector.tensor_scalar(t[:], acc[g, a][:], 0.5, None, MULT)
             r0 = TOK * mp + P * a
-            nc.sync.dma_start(out=out[r0 : r0 + P, C * k : C * (k + 1)], in_=t[:])
+            step = C // pieces
+            for c in range(0, C, step):
+                cols = slice(c, c + step)
+                if engine == "act":
+                    nc.scalar.activation(out=t[:, cols], in_=acc[g, a][:, cols], func=ACT.Copy, scale=0.5)
+                else:
+                    nc.vector.tensor_scalar(t[:, cols], acc[g, a][:, cols], 0.5, None, MULT)
+                nc.sync.dma_start(out=out[r0 : r0 + P, C * k + c : C * k + c + step], in_=t[:, cols])
 
         big_at, w2_at = {}, {}
         for k in range(B):
@@ -352,10 +353,13 @@ def tile_monarch_glu_input_gradient_f3_kernel(tc, dy, w2, z, v, wa, wb, out):
                 transpose_zv(j + 2)
             g, a = divmod(j - LAG, 2)
             if j >= LAG:
-                stage2(g, a, (0, 1))
+                stage2(g, a, PASSES)
+            if last:
+                stage2(6, 0, PASSES, "zT")
+                stage2(6, 1, PASSES, "vT")
             vec_e(j)
             if j > 0:
-                make_dz(j - 1, (nc.gpsimd,))
+                make_dz(j - 1, "dzb", nc.gpsimd, 0, TOK)
                 for key in w2_now:
                     copy_w2(*key, (("gp", W2_GP),))
             if not last:
@@ -366,6 +370,9 @@ def tile_monarch_glu_input_gradient_f3_kernel(tc, dy, w2, z, v, wa, wb, out):
             if not last:
                 vec_h(j + 1)
             vec_dv(j)
+            if last:
+                make_dz(j, "dzlast", nc.vector, 0, P)
+                quant_mid(j - 1, dzb, dzq, "dz")
             if j == 0:
                 transpose_zv(2)
                 act_sp(2)
@@ -377,6 +384,9 @@ def tile_monarch_glu_input_gradient_f3_kernel(tc, dy, w2, z, v, wa, wb, out):
                 act_th(j + 2)
             if j >= LAG:
                 finish(g, a)
+            if last:
+                finish(6, 0)
+                finish(6, 1)
             if j == 0:
                 copy_dy(1, 1, 1, bank, "vec")
             for key in w2_now:
@@ -392,21 +402,15 @@ def tile_monarch_glu_input_gradient_f3_kernel(tc, dy, w2, z, v, wa, wb, out):
             if j == 0:
                 for lh in range(2):
                     quant_dy(1, 1 - lh)
-            if j > 0:
-                quant_mid(j - 1, dzb, dzq, "dz")
             if last:
-                make_dz(j, (nc.vector,))
+                make_dz(j, "dzlast", nc.vector, P, TOK)
                 quant_mid(j, dzb, dzq, "dz", 2)
+            elif j > 0:
+                quant_mid(j - 1, dzb, dzq, "dz")
             big_todo = big_now
             emit_loads(j + 3)
-        stage2(6, 0, (0, 1))
-        stage2(6, 1, (0, 1), "vT")
-        stage2(7, 0, (0,), "zT")
-        stage2(7, 1, (0,), "zT")
-        finish(6, 0)
-        finish(6, 1)
-        for ab in (1, 0):
+        for p in PASSES:
             for a in range(2):
-                stage2(7, a, (1,), parts=(ab,))
-        finish(7, 0, "act")
-        finish(7, 1, "vec")
+                stage2(7, a, [p], ("zT", "vT")[a])
+        finish(7, 0, "act", TAIL)
+        finish(7, 1, "vec", TAIL)

from contextlib import ExitStack

import concourse.mybir as mybir
from concourse.masks import make_identity

M, B, S, Q, C = 512, 4, 512, 1024, 512

F32 = mybir.dt.float32
BF16 = mybir.dt.bfloat16
U32 = mybir.dt.uint32
U8 = mybir.dt.uint8
E4M3 = mybir.dt.float8_e4m3fn_x4
E5M2 = mybir.dt.float8_e5m2_x4
ADD = mybir.AluOpType.add
SUB = mybir.AluOpType.subtract
MULT = mybir.AluOpType.mult
ACT = mybir.ActivationFunctionType

FLOPS = 2 * M * B * S * Q + 2 * 2 * M * B * Q * C

P = 128
PACK = 4
TOK = 256
BUFS = {"zT": 3, "vT": 2, "dh": 2, "dx": 1}
UNITS = [(k, mp, h) for k in range(B) for mp in range(2) for h in range(2)]
LAG = 4
PASSES = [(0, 1), (0, 0), (1, 1), (1, 0)]
TAIL = 2
W2_GP = 96
BIG_ACT = 512


def tile_monarch_glu_input_gradient_f3_kernel(tc, dy, w2, z, v, wa, wb, out):
    nc = tc.nc
    with ExitStack() as ctx:
        const = ctx.enter_context(tc.tile_pool(name="const", bufs=1))
        raw = ctx.enter_context(tc.tile_pool(name="raw", bufs=2))
        inter = ctx.enter_context(tc.tile_pool(name="inter", bufs=3))
        quant = ctx.enter_context(tc.tile_pool(name="quant", bufs=2))
        mid = ctx.enter_context(tc.tile_pool(name="mid", bufs=2))
        psum = ctx.enter_context(tc.psum_pool(name="psum", bufs=2))
        ctx.enter_context(tc.manual_schedule())

        dy_raw, w2_raw, big_raw, zv_raw = {}, {}, {}, {}

        def load_dy(mp):
            t = raw.tile([P, 2, B * S], BF16, name="dyraw", bufs=2)
            for a in range(2):
                r0 = TOK * mp + P * a
                nc.sync.dma_start(out=t[:, a, :], in_=dy[r0 : r0 + P, :])
            dy_raw[mp] = t

        def load_zv(g):
            k, mp = divmod(g, 2)
            pair = []
            for nm, src in (("zraw", z), ("vraw", v)):
                t = raw.tile([P, 2, Q], BF16, name=nm, bufs=3)
                nc.sync.dma_start(
                    out=t[:],
                    in_=src[TOK * mp : TOK * (mp + 1), Q * k : Q * (k + 1)].rearrange("(a p) n -> p a n", p=P),
                )
                pair.append(t)
            zv_raw[g] = pair

        def load_w2(k, l):
            t = raw.tile([P, PACK, TOK], BF16, name="w2raw", bufs=6)
            nc.sync.dma_start(out=t[:], in_=w2[l, :, TOK * k : TOK * (k + 1)].rearrange("(p t) r -> p t r", t=PACK))
            w2_raw[k, l] = t

        def load_big(k, u):
            h, ab = divmod(u, 2)
            t = raw.tile([P, PACK, C], BF16, name="bigraw", bufs=5)
            src = (wa, wb)[ab]
            nc.sync.dma_start(out=t[:], in_=src[k, 512 * h : 512 * (h + 1), :].rearrange("(p t) c -> p t c", t=PACK))
            big_raw[k, u] = t

        def interleave(engine, dst, src, sign):
            if engine == "gp":
                nc.gpsimd.tensor_scalar(dst, src.rearrange("p t c -> p c t"), sign, 0.0, MULT, ADD)
                return
            d = dst.rearrange("p (c i) t -> p c t i", i=4)
            s = src.rearrange("p t (c i) -> p c t i", i=4)
            if engine == "act" and sign > 0:
                nc.scalar.copy(out=d, in_=s)
            elif engine == "act":
                nc.scalar.mul(out=d, in_=s, mul=sign)
            elif sign > 0:
                nc.vector.tensor_copy(out=d, in_=s)
            else:
                nc.vector.tensor_scalar(d, s, sign, None, MULT)

        w2_int, big_int, dy_int = {}, {}, {}
        w2_codes, w2_scales, big_q = {}, {}, {}
        dy_codes = const.tile([P, 2, B, TOK], U32, align_bytes=64, name="dycodes")
        dy_scales = const.tile([P, 2, B, TOK], U8, align_bytes=64, name="dyscales")

        def copy_w2(k, l, shares, c0=0):
            if c0 == 0:
                w2_int[k, l] = inter.tile(
                    [P, TOK, PACK], BF16, align_bytes=64, name="w2int" if 4 * k + l > 4 else "w2int0", bufs=1 if 4 * k + l > 4 else 4
                )
            for engine, width in shares:
                cols = slice(c0, c0 + width)
                interleave(engine, w2_int[k, l][:, cols, :], w2_raw[k, l][:, :, cols], 1.0)
                c0 += width

        def quant_w2(k, l):
            if l == 0:
                w2_codes[k] = quant.tile([P, B, TOK], U32, align_bytes=64, name="w2codes", bufs=2)
                w2_scales[k] = quant.tile([P, B, TOK], U8, align_bytes=64, name="w2scales", bufs=2)
            nc.vector.quantize_mx(
                out=w2_codes[k][:, l, :].bitcast(E4M3),
                scales=w2_scales[k][:, l, :],
                in_=w2_int[k, l][:].rearrange("p r t -> p (r t)"),
            )

        def copy_big(k, u, engine, c0, c1):
            if c0 == 0:
                big_int[k, u] = inter.tile([P, C, PACK], BF16, align_bytes=64, name="bigint", bufs=4)
            if c1 > c0:
                sign = 1.0 if u % 2 else -1.0
                interleave(engine, big_int[k, u][:, c0:c1, :], big_raw[k, u][:, :, c0:c1], sign)

        def quant_big(k, u):
            codes = quant.tile([P, C], U32, align_bytes=64, name="bigcodes", bufs=8)
            scales = quant.tile([P, C], U8, align_bytes=64, name="bigscales", bufs=8)
            nc.vector.quantize_mx(
                out=codes[:].bitcast(E4M3), scales=scales[:], in_=big_int[k, u][:].rearrange("p c t -> p (c t)")
            )
            big_q[k, u] = (codes, scales)

        def transpose_dy(mp, a, lh, tag):
            t = psum.tile([P, PACK, P], F32, name=tag, bufs=BUFS[tag])
            words = dy_raw[mp][:].bitcast(F32)
            for j in range(PACK):
                nc.tensor.transpose(t[:, j, :], words[:, a, 2 * j + lh : B * S // 2 : 8], ident[:])
            return t

        def copy_dy(mp, a, lh, bank, engine):
            if a == 0:
                dy_int[mp, lh] = inter.tile([P, 2, TOK, PACK], BF16, align_bytes=64, name="dyint", bufs=4)
            d = dy_int[mp, lh][:, :, P * a : P * (a + 1), :]
            s = bank[:].bitcast(BF16).rearrange("p t (m e) -> p e m t", e=2)
            if engine == "act":
                nc.scalar.copy(out=d, in_=s)
            else:
                nc.vector.tensor_copy(out=d, in_=s)

        def quant_dy(mp, lh):
            ls = slice(2 * lh, 2 * lh + 2)
            nc.vector.quantize_mx(
                out=dy_codes[:, mp, ls, :].rearrange("p l m -> p (l m)").bitcast(E4M3),
                scales=dy_scales[:, mp, ls, :].rearrange("p l m -> p (l m)"),
                in_=dy_int[mp, lh][:].rearrange("p e m t -> p (e m t)"),
            )

        zT, vT, th, sp, hh, ee, dh = {}, {}, {}, {}, {}, {}, {}
        dzb, dvb, dzq, dvq, acc = {}, {}, {}, {}, {}

        def transpose_zv(i):
            k, mp, h = UNITS[i]
            pair = zv_raw[2 * k + mp]
            for src, tag, keep in ((pair[0], "zT", zT), (pair[1], "vT", vT)):
                t = psum.tile([P, 2, TOK], F32, name=tag, bufs=BUFS[tag])
                words = src[:].bitcast(F32)
                for a in range(2):
                    for u in range(2):
                        nc.tensor.transpose(
                            t[:, u, P * a : P * (a + 1)],
                            words[:, a, 256 * h + u : 256 * (h + 1) : 2],
                            ident[:],
                        )
                keep[i] = t

        def act_sp(i):
            t = mid.tile([P, 2, 2 * TOK], F32, name="sp", bufs=3)
            nc.scalar.activation(out=t[:], in_=zT[i][:].bitcast(BF16), func=ACT.Silu, scale=-1.0)
            sp[i] = t

        def act_th(i):
            t = mid.tile([P, TOK, 2, 2], F32, name="th", bufs=3)
            nc.scalar.activation(
                out=t[:], in_=zT[i][:].bitcast(BF16).rearrange("p u (m e) -> p m u e", e=2), func=ACT.Tanh, scale=0.5
            )
            th[i] = t

        def vec_h(i):
            t = mid.tile([P, 2, 2 * TOK], F32, name="hh", bufs=3)
            nc.vector.scalar_tensor_tensor(
                out=t[:], in0=sp[i][:], scalar=1.0, in1=vT[i][:].bitcast(BF16), op0=SUB, op1=MULT
            )
            hh[i] = t

        def stage1(i):
            k, mp, h = UNITS[i]
            for a in range(2):
                t = psum.tile([P, PACK, P], F32, name="dh", bufs=2)
                cols = slice(P * a, P * (a + 1))
                for l in range(PACK):
                    nc.tensor.matmul_mx(
                        out=t[:, l, :],
                        lhsT=w2_codes[k][:, l, P * h : P * (h + 1)].bitcast(E4M3),
                        lhsT_scale=w2_scales[k][:, l, P * h : P * (h + 1)],
                        rhs=dy_codes[:, mp, l, cols].bitcast(E4M3),
                        rhs_scale=dy_scales[:, mp, l, cols],
                        start=True,
                        stop=True,
                    )
                dh[i, a] = t

        def vec_e(i):
            t = mid.tile([P, TOK, 2, 2], F32, name="ee", bufs=2)
            for a in range(2):
                rows = slice(P * a, P * (a + 1))
                nc.vector.scalar_tensor_tensor(
                    out=t[:, rows].rearrange("p m u e -> p m (u e)"),
                    in0=th[i][:, rows].rearrange("p m u e -> p m (u e)"),
                    scalar=1.0,
                    in1=dh[i, a][:].rearrange("p l m -> p m l"),
                    op0=ADD,
                    op1=MULT,
                )
            ee[i] = t

        def make_dz(i, name, engine, m0, m1):
            if m0 == 0:
                dzb[i] = mid.tile([P, TOK, 2, 2], BF16, align_bytes=64, name=name, bufs=1)
            engine.tensor_tensor(
                out=dzb[i][:, m0:m1],
                in0=ee[i][:, m0:m1],
                in1=hh[i][:, :, 2 * m0 : 2 * m1].rearrange("p u (m e) -> p m u e", e=2),
                op=MULT,
            )

        def vec_dv(i):
            t = mid.tile([P, TOK, 2, 2], BF16, align_bytes=64, name="dvb", bufs=2)
            nc.vector.tensor_tensor(
                out=t[:], in0=ee[i][:], in1=zT[i][:].bitcast(BF16).rearrange("p u (m e) -> p m u e", e=2), op=MULT
            )
            dvb[i] = t

        def quant_mid(i, src, keep, nm, pieces=1):
            codes = quant.tile([P, TOK], U32, align_bytes=64, name=nm + "codes", bufs=6)
            scales = quant.tile([P, TOK], U8, align_bytes=64, name=nm + "scales", bufs=6)
            step = TOK // pieces
            for c in range(0, TOK, step):
                nc.vector.quantize_mx(
                    out=codes[:, c : c + step].bitcast(E5M2),
                    scales=scales[:, c : c + step],
                    in_=src[i][:, c : c + step].rearrange("p m u e -> p (m u e)"),
                )
            keep[i] = (codes, scales)

        def stage2(g, a, passes, tag="dx"):
            k = g // 2
            if passes[0] == (0, 1):
                acc[g, a] = psum.tile([P, C], F32, name=tag, bufs=BUFS[tag])
            cols = slice(P * a, P * (a + 1))
            for h, ab in passes:
                codes, scales = (dzq, dvq)[ab][2 * g + h]
                w_codes, w_scales = big_q[k, 2 * h + ab]
                nc.tensor.matmul_mx(
                    out=acc[g, a][:],
                    lhsT=codes[:, cols].bitcast(E5M2),
                    lhsT_scale=scales[:, cols],
                    rhs=w_codes[:].bitcast(E4M3),
                    rhs_scale=w_scales[:],
                    start=((h, ab) == (0, 1)),
                    stop=((h, ab) == (1, 0)),
                )

        def finish(g, a, engine="act", pieces=1):
            k, mp = divmod(g, 2)
            t = mid.tile([P, C], F32, name="dxo", bufs=4)
            r0 = TOK * mp + P * a
            step = C // pieces
            for c in range(0, C, step):
                cols = slice(c, c + step)
                if engine == "act":
                    nc.scalar.activation(out=t[:, cols], in_=acc[g, a][:, cols], func=ACT.Copy, scale=0.5)
                else:
                    nc.vector.tensor_scalar(t[:, cols], acc[g, a][:, cols], 0.5, None, MULT)
                nc.sync.dma_start(out=out[r0 : r0 + P, C * k + c : C * k + c + step], in_=t[:, cols])

        big_at, w2_at = {}, {}
        for k in range(B):
            for u in range(4):
                big_at[k, u] = 4 * k - 1 + u if k > 0 else min(u, 2)
                if k > 0:
                    w2_at[k, u] = max(0, 4 * k - 5 + u)
        needs = []
        for g in range(2, 2 * B):
            needs.append((2 * g - 2, 0, load_zv, (g,)))
        for key, j in big_at.items():
            needs.append((j, 2, load_big, key))
        for key, j in w2_at.items():
            needs.append((j, 1, load_w2, key))
        needs.sort(key=lambda n: (n[0], n[1], n[3]))

        def emit_loads(upto):
            while needs and needs[0][0] <= upto:
                n = needs[0]
                needs.remove(n)
                n[2](*n[3])

        load_dy(0)
        for l in range(B):
            load_w2(0, l)
        load_zv(0)
        load_dy(1)
        load_zv(1)
        emit_loads(2)

        ident = const.tile([P, P], F32, name="ident")
        make_identity(nc, ident[:])
        warm = const.tile([P, 1], F32, name="warm")
        nc.vector.memset(warm[:], 0.0)
        warm2 = const.tile([P, 1], F32, name="warm2")
        nc.scalar.activation(out=warm2[:], in_=warm[:], func=ACT.Silu)

        pieces = [(a, lh) for a in range(2) for lh in range(2)]
        for a, lh in pieces:
            copy_dy(0, a, lh, transpose_dy(0, a, lh, ("zT", "vT")[lh]), ("vec", "act")[lh])
            if lh == 1:
                copy_w2(0, a, ((("vec", "gp")[a], TOK),))
        copy_w2(0, 2, (("act", TOK),))
        quant_w2(0, 0)
        copy_w2(0, 3, (("vec", TOK),))
        for lh in range(2):
            quant_dy(0, lh)
        for l in range(1, B):
            quant_w2(0, l)
        for i in range(2):
            transpose_zv(i)
            act_sp(i)
            act_th(i)
        stage1(0)
        vec_h(0)
        for a, lh in pieces[:2]:
            copy_dy(1, a, lh, transpose_dy(1, a, lh, ("dx", "zT")[lh]), "act")

        n_units = len(UNITS)
        big_todo = []
        for j in range(n_units):
            last = j == n_units - 1
            w2_now = [key for key, it in w2_at.items() if it == j]
            big_now = [key for key, it in big_at.items() if it == j]
            if last:
                for key in big_todo:
                    quant_big(*key)
                big_todo = []
            if 0 < j < n_units - 2:
                transpose_zv(j + 2)
            g, a = divmod(j - LAG, 2)
            if j >= LAG:
                stage2(g, a, PASSES)
            if last:
                stage2(6, 0, PASSES, "zT")
                stage2(6, 1, PASSES, "vT")
            vec_e(j)
            if j > 0:
                make_dz(j - 1, "dzb", nc.gpsimd, 0, TOK)
                for key in w2_now:
                    copy_w2(*key, (("gp", W2_GP),))
            if not last:
                stage1(j + 1)
            if j == 0:
                bank = transpose_dy(1, 1, 1, "vT")
                copy_dy(1, 1, 0, transpose_dy(1, 1, 0, "dx"), "act")
            if not last:
                vec_h(j + 1)
            vec_dv(j)
            if last:
                make_dz(j, "dzlast", nc.vector, 0, P)
                quant_mid(j - 1, dzb, dzq, "dz")
            if j == 0:
                transpose_zv(2)
                act_sp(2)
                act_th(2)
            for key in big_now:
                copy_big(*key, "act", 0, BIG_ACT)
            if 0 < j < n_units - 2:
                act_sp(j + 2)
                act_th(j + 2)
            if j >= LAG:
                finish(g, a)
            if last:
                finish(6, 0)
                finish(6, 1)
            if j == 0:
                copy_dy(1, 1, 1, bank, "vec")
            for key in w2_now:
                c0 = W2_GP if j > 0 else 0
                copy_w2(*key, (("vec", TOK - c0),), c0)
            for key in big_now:
                copy_big(*key, "vec", BIG_ACT, C)
            quant_mid(j, dvb, dvq, "dv")
            for key in big_todo:
                quant_big(*key)
            for key in w2_now:
                quant_w2(*key)
            if j == 0:
                for lh in range(2):
                    quant_dy(1, 1 - lh)
            if last:
                make_dz(j, "dzlast", nc.vector, P, TOK)
                quant_mid(j, dzb, dzq, "dz", 2)
            elif j > 0:
                quant_mid(j - 1, dzb, dzq, "dz")
            big_todo = big_now
            emit_loads(j + 3)
        for p in PASSES:
            for a in range(2):
                stage2(7, a, [p], ("zT", "vT")[a])
        finish(7, 0, "act", TAIL)
        finish(7, 1, "vec", TAIL)
